import numpy as np, ml_dtypes
CORES = [19,27,51,107,147,155,179,235,275,283,307,363,403,411,435,491]
N = 16
TK, LAY = 512, 4
def setup_inputs(rng):
    return {"x": rng.standard_normal((N, 128, TK), dtype=np.float32).astype(ml_dtypes.bfloat16), "wu": (rng.standard_normal((N, 128, LAY * 256), dtype=np.float32) / 16).astype(ml_dtypes.bfloat16), "wd": (rng.standard_normal((N, 128, 256), dtype=np.float32) / 16).astype(ml_dtypes.bfloat16)}
def setup_inputs_big(rng):
    d = setup_inputs(rng)
    for k in ("x",): d[k] = (d[k].astype(np.float32) * 1048576.0).astype(d[k].dtype)
    return d
def setup_inputs_small(rng):
    d = setup_inputs(rng)
    for k in ("x",): d[k] = (d[k].astype(np.float32) * (1 / 1048576.0)).astype(d[k].dtype)
    return d
def setup_inputs_apart(rng):
    d = setup_inputs(rng)
    f = (10.0 ** rng.permutation(np.linspace(-1.5, 1.5, N))).astype(np.float32).reshape(N, 1, 1)
    for k in ("x",): d[k] = (d[k].astype(np.float32) * f).astype(d[k].dtype)
    return d
def reference(x, wu, wd):
    X, WU, WD = x.astype(np.float64), wu.astype(np.float64), wd.astype(np.float64)
    s = list(X)
    for l in range(LAY):
        for q in range(0, N, 2 << l):
            p = q + (1 << l)
            s[q] = np.maximum(WU[q][:, 256 * l:256 * l + 128].T @ s[q] + WU[q][:, 256 * l + 128:256 * l + 256].T @ s[p], 0.0)
    for l in range(LAY - 1, -1, -1):
        for q in range(0, N, 2 << l):
            p = q + (1 << l)
            s[p] = np.maximum(WD[p][:, 0:128].T @ s[p] + WD[p][:, 128:256].T @ s[q], 0.0)
    return {"y": np.stack(s).astype(ml_dtypes.bfloat16)}

@@ -1,0 +1,216 @@
+from concourse.mybir import AluOpType
+
+TK = 512
+NCH = 2
+CW = TK // NCH
+NODES = ["a", "s2", "h", "ar", "rt", "s8", "sq", "sp", "lf"]
+
+
+def _bf(cols):
+    return ("sbuf", [128, cols], "bfloat16")
+
+
+SCRATCH = {
+    "xs": _bf(TK), "wus": _bf(512), "wds": _bf(256), "zeros": ("sbuf", [128, CW], "float32"),
+    "x1": _bf(TK), "x2": _bf(TK), "x3": _bf(TK), "w2": _bf(256), "d2": _bf(256),
+    "wt": _bf(768), "hp": _bf(TK), "ao": _bf(TK),
+    "a": _bf(TK), "s2": _bf(TK), "h": _bf(TK), "ar": _bf(TK), "rt": _bf(TK), "s8": _bf(TK), "sq": _bf(TK),
+    "sp": _bf(TK), "land": _bf(TK), "yo": _bf(TK),
+}
+for _i in range(8):
+    SCRATCH["ps%d" % _i] = ("psum", [128, 512], "float32")
+
+SEMAPHORES = ["ld_x", "ld_w", "ld_d", "ld_wt", "z", "sent", "st",
+              "r_x1", "r_x2", "r_x3", "r_w2", "r_d2", "r_wa", "r_wb", "r_wc", "r_hp", "r_ao", "r_land"]
+for _n in NODES:
+    for _c in range(NCH):
+        SEMAPHORES += ["p_%s%d" % (_n, _c), "v_%s%d" % (_n, _c)]
+
+
+def rank_program(g, core, T, topo):
+    rank = T.rank_of(core)
+    if rank is None:
+        return
+    cores, sem = T.cores, T.sem
+    queues = {"g": g, "pe": g.tensor, "dve": g.vector, "sy": g.sync, "sc": g.scalar}
+    seen, sent, loaded = {}, [0], {}
+
+    def engines(src, dst):
+        return bin(topo.mask(cores[src], cores[dst])).count("1")
+
+    def wait(qn, s, v):
+        if seen.get((qn, s), 0) < v:
+            seen[(qn, s)] = v
+            queues[qn].wait_ge(sem[s], v)
+
+    def load(qn, out, in_, s):
+        queues[qn].dma_start(out, in_).then_inc(sem[s], 16)
+        loaded[s] = loaded.get(s, 0) + 16
+
+    def send(dst, out, in_, s):
+        rid, pid = topo.addr(cores[dst], core)
+        g.remote_dma(out_ap=out, in_ap=in_, remote_sem=sem[s], local_sem=sem.sent, pid=pid, routing_id=rid,
+                     dma_engine_mask=topo.mask(core, cores[dst]))
+        sent[0] += engines(rank, dst)
+
+    def after(qn, node):
+        for c in range(NCH):
+            wait(qn, "v_%s%d" % (node, c), 1)
+
+    def mm(node, pair, lhsT, rhs, start, stop, deps=(), src=None):
+        for c in range(NCH):
+            for s, v in deps:
+                wait("pe", s, v)
+            if src is not None:
+                wait("pe", "v_%s%d" % (src, c), 1)
+            ins = g.tensor.matmul(T["ps%d" % (pair * NCH + c)][:, 0:CW], lhsT, rhs[:, c * CW:(c + 1) * CW], start, stop)
+            if stop:
+                ins.then_inc(sem["p_%s%d" % (node, c)], 1)
+
+    def relu(node, pair, out):
+        wait("dve", "z", 1)
+        for c in range(NCH):
+            wait("dve", "p_%s%d" % (node, c), 1)
+            g.vector.tensor_tensor(out[:, c * CW:(c + 1) * CW], T["ps%d" % (pair * NCH + c)][:, 0:CW], T.zeros[:, 0:CW],
+                                   AluOpType.max).then_inc(sem["v_%s%d" % (node, c)], 1)
+
+    def store(buf):
+        g.sync.dma_start(T.y[:], buf[:]).then_inc(sem.st, 16)
+        g.sync.wait_ge(sem.st, 16)
+
+    mine = [r for r in range(len(cores)) if topo.host(cores[r]) == topo.host(core)]
+    q, role = mine[0], mine.index(rank)
+    centres = sorted({min(r for r in range(len(cores)) if topo.host(cores[r]) == topo.host(c)) for c in cores})
+
+    if role != 0:
+        if role == 2:
+            load("sy", T.wus[:, 0:256], T.wu[:, 0:256], "ld_w")
+            load("sc", T.xs[:], T.x[:], "ld_x")
+            load("sy", T.wds[:], T.wd[:], "ld_d")
+            wait("g", "ld_w", 16)
+            send(q, T.w2[:], T.wus[:, 0:256], "r_w2")
+            wait("g", "ld_x", 16)
+            send(q, T.x2[:], T.xs[:], "r_x2")
+            wait("g", "ld_d", 16)
+            send(q, T.d2[:], T.wds[:], "r_d2")
+            wait("sy", "r_land", engines(q, rank))
+            store(T.land)
+        else:
+            load("sy", T.xs[:], T.x[:], "ld_x")
+            load("sc", T.wds[:], T.wd[:], "ld_d")
+            g.vector.memset(T.zeros[:], 0.0).then_inc(sem.z, 1)
+            wait("g", "ld_x", 16)
+            send(q, T["x%d" % role][:], T.xs[:], "r_x%d" % role)
+            mm("lf", 0, T.wds[:, 0:128], T.xs, True, False, deps=[("ld_d", 16), ("ld_x", 16)])
+            mm("lf", 0, T.wds[:, 128:256], T.land, False, True, deps=[("r_land", engines(q, rank))])
+            relu("lf", 0, T.yo)
+            after("sy", "lf")
+            store(T.yo)
+        wait("g", "sent", sent[0])
+        return
+
+    top, low = centres[0], centres[len(centres) // 2]
+    half = len(cores) // 2
+    pair_root = q - q % half
+    partner = [c for c in centres if c != q and c // half == q // half][0]
+    cable = [c for c in centres if c // half != q // half and topo.may_write(core, cores[c])][0]
+    far = [c for c in centres if c != top and not topo.may_write(cores[top], cores[c])]
+    near = [c for c in centres if c != top and c not in far]
+    D8, E8 = T.wt[:, 0:128], T.wt[:, 128:256]
+    U2, V2 = T.wt[:, 256:384], T.wt[:, 384:512]
+    U3, V3 = T.wt[:, 512:640], T.wt[:, 640:768]
+
+    g.vector.memset(T.zeros[:], 0.0).then_inc(sem.z, 1)
+    if q == top:
+        load("sy", T.wt[:, 256:768], T.wu[:, 512:1024], "ld_wt")
+        load("sc", T.wus[:], T.wu[:, 0:512], "ld_w")
+        load("sy", T.xs[:], T.x[:], "ld_x")
+    elif q == low:
+        load("sy", T.wt[:, 256:512], T.wu[:, 512:768], "ld_wt")
+        load("sc", T.wus[:], T.wu[:, 0:512], "ld_w")
+        load("sy", T.xs[:], T.x[:], "ld_x")
+        load("sc", T.wt[:, 0:256], T.wd[:], "ld_d")
+    else:
+        load("sy", T.xs[:], T.x[:], "ld_x")
+        load("sc", T.wus[:], T.wu[:, 0:512], "ld_w")
+        load("sy", T.wds[:], T.wd[:], "ld_d")
+
+    if q == top:
+        have2 = have3 = [("ld_wt", loaded["ld_wt"])]
+        have8 = []
+    elif q == low:
+        have2, have8 = [("ld_wt", loaded["ld_wt"])], [("ld_d", loaded["ld_d"])]
+        have3 = [("r_wa", sum(engines(n, q) for n in near))]
+    else:
+        have3 = [("r_wa", engines(top, q))]
+        have2 = have3 if pair_root == top else [("r_wb", engines(low, q))]
+        have8 = [] if pair_root == top else [("r_wc", engines(low, q))]
+
+    if q == top:
+        wait("g", "ld_wt", loaded["ld_wt"])
+        for n in near:
+            if n != partner:
+                send(n, T.wt[:, 512:768], T.wt[:, 512:768], "r_wa")
+        send(partner, T.wt[:, 256:768], T.wt[:, 256:768], "r_wa")
+    elif q == low:
+        wait("g", "ld_wt", loaded["ld_wt"])
+        send(partner, T.wt[:, 256:512], T.wt[:, 256:512], "r_wb")
+    else:
+        wait("g", "r_wa", engines(top, q))
+        i = near.index(q)
+        for f in far:
+            send(f, T.wt[:, 512 + 128 * i:640 + 128 * i], T.wt[:, 512 + 128 * i:640 + 128 * i], "r_wa")
+    after("g", "h")
+    send(partner, T.hp[:], T.h[:], "r_hp")
+    if q == low:
+        wait("g", "ld_d", loaded["ld_d"])
+        send(partner, T.wt[:, 0:256], T.wt[:, 0:256], "r_wc")
+    after("g", "ar")
+    send(cable, T.ao[:], T.ar[:], "r_ao")
+
+    in_low = pair_root == low
+    own_node = q != pair_root
+    sqn = "sq" if own_node else ("s8" if in_low else "rt")
+    after("g", sqn)
+    send(mine[1], T.land[:], T[sqn][:], "r_land")
+    after("g", "sp")
+    send(mine[3], T.land[:], T.sp[:], "r_land")
+    send(mine[2], T.land[:], T.sp[:], "r_land")
+    wait("g", "sent", sent[0])
+
+    mm("a", 0, T.wus[:, 0:128], T.xs, True, False, deps=[("ld_w", 16), ("ld_x", 16)])
+    mm("a", 0, T.wus[:, 128:256], T.x1, False, True, deps=[("r_x1", engines(mine[1], q))])
+    mm("s2", 1, T.w2[:, 128:256], T.x3, True, False,
+       deps=[("r_w2", engines(mine[2], q)), ("r_x3", engines(mine[3], q))])
+    mm("h", 2, T.wus[:, 256:384], T.a, True, False, src="a")
+    mm("s2", 1, T.w2[:, 0:128], T.x2, False, True, deps=[("r_x2", engines(mine[2], q))])
+    mm("h", 2, T.wus[:, 384:512], T.s2, False, True, src="s2")
+    mm("ar", 3, V2 if own_node else U2, T.h, True, False, deps=have2, src="h")
+    if own_node:
+        mm("sq", 0, T.wds[:, 0:128], T.h, True, False, deps=[("ld_d", 16)], src="h")
+    mm("sp", 1, T.d2[:, 0:128], T.s2, True, False, deps=[("r_d2", engines(mine[2], q))], src="s2")
+    mm("ar", 3, U2 if own_node else V2, T.hp, False, True, deps=[("r_hp", engines(partner, q))])
+    mm("rt", 2, V3 if in_low else U3, T.ar, True, False, deps=have3, src="ar")
+    if in_low:
+        mm("s8", 3, D8, T.ar, True, False, deps=have8, src="ar")
+    mm("rt", 2, U3 if in_low else V3, T.ao, False, True, deps=[("r_ao", engines(cable, q))])
+    if in_low:
+        mm("s8", 3, E8, T.rt, False, True, src="rt")
+    if own_node:
+        up = "s8" if in_low else "rt"
+        mm("sq", 0, T.wds[:, 128:256], T[up], False, True, src=up)
+    mm("sp", 1, T.d2[:, 128:256], T[sqn], False, True, src=sqn)
+
+    relu("a", 0, T.a)
+    relu("s2", 1, T.s2)
+    relu("h", 2, T.h)
+    relu("ar", 3, T.ar)
+    relu("rt", 2, T.rt)
+    if in_low:
+        relu("s8", 3, T.s8)
+    if own_node:
+        relu("sq", 0, T.sq)
+    relu("sp", 1, T.sp)
+
+    after("sy", sqn)
+    store(T[sqn])

@@ -16,14 +16,16 @@ SCRATCH = {
     "wt": _bf(768), "hp": _bf(TK), "ao": _bf(TK),
     "a": _bf(TK), "s2": _bf(TK), "h": _bf(TK), "ar": _bf(TK), "rt": _bf(TK), "s8": _bf(TK), "sq": _bf(TK),
     "sp": _bf(TK), "land": _bf(TK), "yo": _bf(TK),
+    "yl": ("dram", [128, TK], "bfloat16"),
 }
 for _i in range(8):
     SCRATCH["ps%d" % _i] = ("psum", [128, 512], "float32")
 
-SEMAPHORES = ["ld_x", "ld_w", "ld_d", "ld_wt", "z", "sent", "st",
-              "r_x1", "r_x2", "r_x3", "r_w2", "r_d2", "r_wa", "r_wb", "r_wc", "r_hp", "r_ao", "r_land"]
-for _n in NODES:
-    for _c in range(NCH):
+SEMAPHORES = ["ld_x", "ld_w", "ld_d", "ld_wt", "ld_u3", "ld_v3", "z", "sent", "st",
+              "r_w2", "r_d2", "r_wa", "r_wb", "r_wc", "r_wd", "r_land"]
+for _c in range(NCH):
+    SEMAPHORES += ["%s%d" % (_n, _c) for _n in ("ld_x", "r_x1_", "r_x2_", "r_x3_", "r_hp", "r_ao", "r_ln")]
+    for _n in NODES:
         SEMAPHORES += ["p_%s%d" % (_n, _c), "v_%s%d" % (_n, _c)]
 
 
@@ -33,7 +35,8 @@ def rank_program(g, core, T, topo):
         return
     cores, sem = T.cores, T.sem
     queues = {"g": g, "pe": g.tensor, "dve": g.vector, "sy": g.sync, "sc": g.scalar}
-    seen, sent, loaded = {}, [0], {}
+    seen, sent = {}, [0]
+    blocks = range(NCH)
 
     def engines(src, dst):
         return bin(topo.mask(cores[src], cores[dst])).count("1")
@@ -45,7 +48,6 @@ def rank_program(g, core, T, topo):
 
     def load(qn, out, in_, s):
         queues[qn].dma_start(out, in_).then_inc(sem[s], 16)
-        loaded[s] = loaded.get(s, 0) + 16
 
     def send(dst, out, in_, s):
         rid, pid = topo.addr(cores[dst], core)
@@ -53,26 +55,24 @@ def rank_program(g, core, T, topo):
                      dma_engine_mask=topo.mask(core, cores[dst]))
         sent[0] += engines(rank, dst)
 
-    def after(qn, node):
-        for c in range(NCH):
-            wait(qn, "v_%s%d" % (node, c), 1)
+    def blk(buf, c):
+        return buf[:, c * CW:(c + 1) * CW]
 
-    def mm(node, pair, lhsT, rhs, start, stop, deps=(), src=None):
-        for c in range(NCH):
-            for s, v in deps:
-                wait("pe", s, v)
-            if src is not None:
-                wait("pe", "v_%s%d" % (src, c), 1)
-            ins = g.tensor.matmul(T["ps%d" % (pair * NCH + c)][:, 0:CW], lhsT, rhs[:, c * CW:(c + 1) * CW], start, stop)
-            if stop:
-                ins.then_inc(sem["p_%s%d" % (node, c)], 1)
+    def done(node, c):
+        return ("v_%s%d" % (node, c), 1)
 
-    def relu(node, pair, out):
+    def mm(node, pair, c, lhsT, rhs, start, stop, deps):
+        for s, v in deps:
+            wait("pe", s, v)
+        ins = g.tensor.matmul(T["ps%d" % (pair * NCH + c)][:, 0:CW], lhsT, blk(rhs, c), start, stop)
+        if stop:
+            ins.then_inc(sem["p_%s%d" % (node, c)], 1)
+
+    def relu(node, pair, c, out):
         wait("dve", "z", 1)
-        for c in range(NCH):
-            wait("dve", "p_%s%d" % (node, c), 1)
-            g.vector.tensor_tensor(out[:, c * CW:(c + 1) * CW], T["ps%d" % (pair * NCH + c)][:, 0:CW], T.zeros[:, 0:CW],
-                                   AluOpType.max).then_inc(sem["v_%s%d" % (node, c)], 1)
+        wait("dve", "p_%s%d" % (node, c), 1)
+        g.vector.tensor_tensor(blk(out, c), T["ps%d" % (pair * NCH + c)][:, 0:CW], T.zeros[:, 0:CW],
+                               AluOpType.max).then_inc(sem["v_%s%d" % (node, c)], 1)
 
     def store(buf):
         g.sync.dma_start(T.y[:], buf[:]).then_inc(sem.st, 16)
@@ -85,26 +85,29 @@ def rank_program(g, core, T, topo):
     if role != 0:
         if role == 2:
             load("sy", T.wus[:, 0:256], T.wu[:, 0:256], "ld_w")
-            load("sc", T.xs[:], T.x[:], "ld_x")
-            load("sy", T.wds[:], T.wd[:], "ld_d")
             wait("g", "ld_w", 16)
             send(q, T.w2[:], T.wus[:, 0:256], "r_w2")
-            wait("g", "ld_x", 16)
-            send(q, T.x2[:], T.xs[:], "r_x2")
+        else:
+            g.vector.memset(T.zeros[:], 0.0).then_inc(sem.z, 1)
+        for c in blocks:
+            load("sc" if (role == 2 or c) else "sy", blk(T.xs, c), blk(T.x, c), "ld_x%d" % c)
+            wait("g", "ld_x%d" % c, 16)
+            send(q, blk(T["x%d" % role], c), blk(T.xs, c), "r_x%d_%d" % (role, c))
+        wait("sc", "sent", sent[0])
+        load("sc", T.wds[:], T.wd[:], "ld_d")
+        if role == 2:
             wait("g", "ld_d", 16)
             send(q, T.d2[:], T.wds[:], "r_d2")
             wait("sy", "r_land", engines(q, rank))
-            store(T.land)
+            store(T.yl)
         else:
-            load("sy", T.xs[:], T.x[:], "ld_x")
-            load("sc", T.wds[:], T.wd[:], "ld_d")
-            g.vector.memset(T.zeros[:], 0.0).then_inc(sem.z, 1)
-            wait("g", "ld_x", 16)
-            send(q, T["x%d" % role][:], T.xs[:], "r_x%d" % role)
-            mm("lf", 0, T.wds[:, 0:128], T.xs, True, False, deps=[("ld_d", 16), ("ld_x", 16)])
-            mm("lf", 0, T.wds[:, 128:256], T.land, False, True, deps=[("r_land", engines(q, rank))])
-            relu("lf", 0, T.yo)
-            after("sy", "lf")
+            for c in blocks:
+                mm("lf", 0, c, T.wds[:, 0:128], T.xs, True, False, [("ld_d", 16), ("ld_x%d" % c, 16)])
+            for c in blocks:
+                mm("lf", 0, c, T.wds[:, 128:256], T.land, False, True,
+                   [("r_ln%d" % c if role == 1 else "r_land", engines(q, rank))])
+                relu("lf", 0, c, T.yo)
+                wait("sy", *done("lf", c))
             store(T.yo)
         wait("g", "sent", sent[0])
         return
@@ -116,101 +119,134 @@ def rank_program(g, core, T, topo):
     cable = [c for c in centres if c // half != q // half and topo.may_write(core, cores[c])][0]
     far = [c for c in centres if c != top and not topo.may_write(cores[top], cores[c])]
     near = [c for c in centres if c != top and c not in far]
-    D8, E8 = T.wt[:, 0:128], T.wt[:, 128:256]
-    U2, V2 = T.wt[:, 256:384], T.wt[:, 384:512]
-    U3, V3 = T.wt[:, 512:640], T.wt[:, 640:768]
+    D8, E8, U3 = T.wt[:, 0:128], T.wt[:, 128:256], T.wt[:, 256:384]
+    U2, V2, V3 = T.wt[:, 384:512], T.wt[:, 512:640], T.wt[:, 640:768]
+    in_low = pair_root == low
+    own_node = q != pair_root
+    sqn = "sq" if own_node else ("s8" if in_low else "rt")
 
     g.vector.memset(T.zeros[:], 0.0).then_inc(sem.z, 1)
     if q == top:
-        load("sy", T.wt[:, 256:768], T.wu[:, 512:1024], "ld_wt")
+        load("sy", U3, T.wu[:, 768:896], "ld_u3")
+        load("sc", V3, T.wu[:, 896:1024], "ld_v3")
+        load("sy", T.wt[:, 384:640], T.wu[:, 512:768], "ld_wt")
         load("sc", T.wus[:], T.wu[:, 0:512], "ld_w")
         load("sy", T.xs[:], T.x[:], "ld_x")
     elif q == low:
-        load("sy", T.wt[:, 256:512], T.wu[:, 512:768], "ld_wt")
-        load("sc", T.wus[:], T.wu[:, 0:512], "ld_w")
+        load("sy", T.wt[:, 384:640], T.wu[:, 512:768], "ld_wt")
         load("sy", T.xs[:], T.x[:], "ld_x")
+        wait("sc", "ld_wt", 16)
+        load("sc", T.wus[:], T.wu[:, 0:512], "ld_w")
         load("sc", T.wt[:, 0:256], T.wd[:], "ld_d")
     else:
         load("sy", T.xs[:], T.x[:], "ld_x")
         load("sc", T.wus[:], T.wu[:, 0:512], "ld_w")
         load("sy", T.wds[:], T.wd[:], "ld_d")
 
+    have8 = []
     if q == top:
-        have2 = have3 = [("ld_wt", loaded["ld_wt"])]
-        have8 = []
+        have2, have3 = [("ld_wt", 16)], [("ld_u3", 16), ("ld_v3", 16)]
     elif q == low:
-        have2, have8 = [("ld_wt", loaded["ld_wt"])], [("ld_d", loaded["ld_d"])]
+        have2, have8 = [("ld_wt", 16)], [("ld_d", 16)]
         have3 = [("r_wa", sum(engines(n, q) for n in near))]
     else:
-        have3 = [("r_wa", engines(top, q))]
-        have2 = have3 if pair_root == top else [("r_wb", engines(low, q))]
-        have8 = [] if pair_root == top else [("r_wc", engines(low, q))]
+        have3 = [("r_wa", engines(top, q)), ("r_wb", engines(top, q))]
+        have2 = [("r_wb", engines(top, q))]
+        if in_low:
+            have2, have8 = [("r_wd", engines(low, q))], [("r_wc", engines(low, q))]
 
     if q == top:
-        wait("g", "ld_wt", loaded["ld_wt"])
-        for n in near:
-            if n != partner:
-                send(n, T.wt[:, 512:768], T.wt[:, 512:768], "r_wa")
-        send(partner, T.wt[:, 256:768], T.wt[:, 256:768], "r_wa")
+        wait("g", "ld_u3", 16)
+        send(partner, U3, U3, "r_wa")
+        wait("g", "ld_v3", 16)
+        send(cable, V3, V3, "r_wa")
+        send(cable, U3, U3, "r_wb")
+        wait("g", "r_w2", engines(mine[2], q))
+        wait("g", "ld_wt", 16)
+        send(partner, T.wt[:, 384:768], T.wt[:, 384:768], "r_wb")
     elif q == low:
-        wait("g", "ld_wt", loaded["ld_wt"])
-        send(partner, T.wt[:, 256:512], T.wt[:, 256:512], "r_wb")
+        wait("g", "ld_wt", 16)
+        send(partner, T.wt[:, 384:640], T.wt[:, 384:640], "r_wd")
     else:
         wait("g", "r_wa", engines(top, q))
-        i = near.index(q)
+        tile = V3 if in_low else U3
         for f in far:
-            send(f, T.wt[:, 512 + 128 * i:640 + 128 * i], T.wt[:, 512 + 128 * i:640 + 128 * i], "r_wa")
-    after("g", "h")
-    send(partner, T.hp[:], T.h[:], "r_hp")
+            send(f, tile, tile, "r_wa")
+    for c in blocks:
+        wait("g", *done("h", c))
+        send(partner, blk(T.hp, c), blk(T.h, c), "r_hp%d" % c)
     if q == low:
-        wait("g", "ld_d", loaded["ld_d"])
+        wait("g", "ld_d", 16)
         send(partner, T.wt[:, 0:256], T.wt[:, 0:256], "r_wc")
-    after("g", "ar")
-    send(cable, T.ao[:], T.ar[:], "r_ao")
-
-    in_low = pair_root == low
-    own_node = q != pair_root
-    sqn = "sq" if own_node else ("s8" if in_low else "rt")
-    after("g", sqn)
-    send(mine[1], T.land[:], T[sqn][:], "r_land")
-    after("g", "sp")
+    for c in blocks:
+        wait("g", *done("ar", c))
+        send(cable, blk(T.ao, c), blk(T.ar, c), "r_ao%d" % c)
+    for c in blocks:
+        wait("g", *done(sqn, c))
+        send(mine[1], blk(T.land, c), blk(T[sqn], c), "r_ln%d" % c)
+    for c in blocks:
+        wait("g", *done("sp", c))
     send(mine[3], T.land[:], T.sp[:], "r_land")
-    send(mine[2], T.land[:], T.sp[:], "r_land")
+    send(mine[2], T.yl[:], T.sp[:], "r_land")
     wait("g", "sent", sent[0])
 
-    mm("a", 0, T.wus[:, 0:128], T.xs, True, False, deps=[("ld_w", 16), ("ld_x", 16)])
-    mm("a", 0, T.wus[:, 128:256], T.x1, False, True, deps=[("r_x1", engines(mine[1], q))])
-    mm("s2", 1, T.w2[:, 128:256], T.x3, True, False,
-       deps=[("r_w2", engines(mine[2], q)), ("r_x3", engines(mine[3], q))])
-    mm("h", 2, T.wus[:, 256:384], T.a, True, False, src="a")
-    mm("s2", 1, T.w2[:, 0:128], T.x2, False, True, deps=[("r_x2", engines(mine[2], q))])
-    mm("h", 2, T.wus[:, 384:512], T.s2, False, True, src="s2")
-    mm("ar", 3, V2 if own_node else U2, T.h, True, False, deps=have2, src="h")
-    if own_node:
-        mm("sq", 0, T.wds[:, 0:128], T.h, True, False, deps=[("ld_d", 16)], src="h")
-    mm("sp", 1, T.d2[:, 0:128], T.s2, True, False, deps=[("r_d2", engines(mine[2], q))], src="s2")
-    mm("ar", 3, U2 if own_node else V2, T.hp, False, True, deps=[("r_hp", engines(partner, q))])
-    mm("rt", 2, V3 if in_low else U3, T.ar, True, False, deps=have3, src="ar")
-    if in_low:
-        mm("s8", 3, D8, T.ar, True, False, deps=have8, src="ar")
-    mm("rt", 2, U3 if in_low else V3, T.ao, False, True, deps=[("r_ao", engines(cable, q))])
-    if in_low:
-        mm("s8", 3, E8, T.rt, False, True, src="rt")
-    if own_node:
-        up = "s8" if in_low else "rt"
-        mm("sq", 0, T.wds[:, 128:256], T[up], False, True, src=up)
-    mm("sp", 1, T.d2[:, 128:256], T[sqn], False, True, src=sqn)
+    def came(leaf, c):
+        return ("r_x%d_%d" % (leaf, c), engines(mine[leaf], q))
 
-    relu("a", 0, T.a)
-    relu("s2", 1, T.s2)
-    relu("h", 2, T.h)
-    relu("ar", 3, T.ar)
-    relu("rt", 2, T.rt)
-    if in_low:
-        relu("s8", 3, T.s8)
-    if own_node:
-        relu("sq", 0, T.sq)
-    relu("sp", 1, T.sp)
+    def a_fin(c):
+        mm("a", 0, c, T.wus[:, 128:256], T.x1, False, True, [came(1, c)])
+        relu("a", 0, c, T.a)
 
-    after("sy", sqn)
+    def s2_pre(c):
+        mm("s2", 1, c, T.w2[:, 128:256], T.x3, True, False, [("r_w2", engines(mine[2], q)), came(3, c)])
+
+    def s2_fin(c):
+        mm("s2", 1, c, T.w2[:, 0:128], T.x2, False, True, [came(2, c)])
+        relu("s2", 1, c, T.s2)
+
+    def h_pre(c):
+        mm("h", 2, c, T.wus[:, 256:384], T.a, True, False, [done("a", c)])
+
+    def h_fin(c):
+        mm("h", 2, c, T.wus[:, 384:512], T.s2, False, True, [done("s2", c)])
+        relu("h", 2, c, T.h)
+
+    for c in blocks:
+        mm("a", 0, c, T.wus[:, 0:128], T.xs, True, False, [("ld_w", 16), ("ld_x", 16)])
+    a_fin(0), s2_pre(0), h_pre(0), s2_fin(0), a_fin(1), s2_pre(1), h_fin(0), h_pre(1), s2_fin(1), h_fin(1)
+
+    for c in blocks:
+        if own_node:
+            mm("sq", 0, c, T.wds[:, 0:128], T.h, True, False, [("ld_d", 16), done("h", c)])
+        mm("ar", 3, c, V2 if own_node else U2, T.h, True, False, have2 + [done("h", c)])
+    for c in blocks:
+        mm("ar", 3, c, U2 if own_node else V2, T.hp, False, True, [("r_hp%d" % c, engines(partner, q))])
+        relu("ar", 3, c, T.ar)
+    for c in blocks:
+        mm("rt", 2, c, V3 if in_low else U3, T.ar, True, False, have3 + [done("ar", c)])
+        if in_low:
+            mm("s8", 3, c, D8, T.ar, True, False, have8 + [done("ar", c)])
+        mm("sp", 1, c, T.d2[:, 0:128], T.s2, True, False, [("r_d2", engines(mine[2], q)), done("s2", c)])
+
+    chain = [("rt", 2, U3 if in_low else V3, T.ao, None)]
+    if in_low:
+        chain.append(("s8", 3, E8, T.rt, "rt"))
+    if own_node:
+        chain.append(("sq", 0, T.wds[:, 128:256], T[chain[-1][0]], chain[-1][0]))
+    chain.append(("sp", 1, T.d2[:, 128:256], T[sqn], sqn))
+    order, nxt = [(0, 0), (1, 0)], [2, 0]
+    while nxt[0] < len(chain) or nxt[1] < len(chain):
+        for c in (1, 0):
+            if nxt[c] < len(chain):
+                order.append((nxt[c], c))
+                nxt[c] += 1
+    for k, c in order:
+        node, pair, tile, operand, src = chain[k]
+        mm(node, pair, c, tile, operand, False, True,
+           [done(src, c)] if src else [("r_ao%d" % c, engines(cable, q))])
+        relu(node, pair, c, T[node])
+
+    for c in blocks:
+        wait("sy", *done(sqn, c))
+    wait("sy", "sent", sent[0])
     store(T[sqn])

@@ -1,9 +1,8 @@
 from concourse.mybir import AluOpType
 
 TK = 512
-NCH = 2
-CW = TK // NCH
-NODES = ["a", "s2", "h", "ar", "rt", "s8", "sq", "sp", "lf"]
+CW = TK // 2
+BANK = {"a": 0, "s2": 1, "h": 2, "ar": 3, "rt": 4, "s8": 5, "sq": 6, "sp": 7, "lf0": 0, "lf1": 1, "q0": 0, "q1": 1}
 
 
 def _bf(cols):
@@ -11,35 +10,33 @@ def _bf(cols):
 
 
 SCRATCH = {
-    "xs": _bf(TK), "wus": _bf(512), "wds": _bf(256), "zeros": ("sbuf", [128, CW], "float32"),
-    "x1": _bf(TK), "x2": _bf(TK), "x3": _bf(TK), "w2": _bf(256), "d2": _bf(256),
-    "wt": _bf(768), "hp": _bf(TK), "ao": _bf(TK),
-    "a": _bf(TK), "s2": _bf(TK), "h": _bf(TK), "ar": _bf(TK), "rt": _bf(TK), "s8": _bf(TK), "sq": _bf(TK),
-    "sp": _bf(TK), "land": _bf(TK), "yo": _bf(TK),
-    "yl": ("dram", [128, TK], "bfloat16"),
+    "xs": _bf(TK), "wus": _bf(512), "wds": _bf(256), "wdo": _bf(256), "zeros": ("sbuf", [128, CW], "float32"),
+    "xo": _bf(CW), "x2": _bf(CW), "x3": _bf(CW), "v2": _bf(128), "d2": _bf(256), "wt": _bf(768),
+    "hp": _bf(CW), "ao": _bf(CW), "a": _bf(CW), "s2": _bf(CW), "h": _bf(CW), "ar": _bf(CW), "rt": _bf(CW),
+    "s8": _bf(CW), "sq": _bf(CW), "sp": _bf(CW), "land": _bf(TK), "yo": _bf(TK), "p2": _bf(TK),
 }
 for _i in range(8):
     SCRATCH["ps%d" % _i] = ("psum", [128, 512], "float32")
 
-SEMAPHORES = ["ld_x", "ld_w", "ld_d", "ld_wt", "ld_u3", "ld_v3", "z", "sent", "st",
-              "r_w2", "r_d2", "r_wa", "r_wb", "r_wc", "r_wd", "r_land"]
-for _c in range(NCH):
-    SEMAPHORES += ["%s%d" % (_n, _c) for _n in ("ld_x", "r_x1_", "r_x2_", "r_x3_", "r_hp", "r_ao", "r_ln")]
-    for _n in NODES:
-        SEMAPHORES += ["p_%s%d" % (_n, _c), "v_%s%d" % (_n, _c)]
+SEMAPHORES = ["ld_x", "ld_x0", "ld_x1", "ld_w0", "ld_w1", "ld_wt", "ld_w8", "ld_d", "ld_o", "z", "sent", "st0", "st1",
+              "r_c", "r_w0", "r_w1", "r_xo", "r_v2", "r_x2", "r_x3", "r_d2", "r_w2t", "r_w3", "r_w8", "r_wds",
+              "r_hp", "r_ao", "r_land", "r_ln0", "r_ln1", "t_s2"]
+for _n in BANK:
+    SEMAPHORES += ["p_" + _n, "v_" + _n]
 
 
 def rank_program(g, core, T, topo):
-    rank = T.rank_of(core)
-    if rank is None:
-        return
     cores, sem = T.cores, T.sem
+    n = len(cores)
+    rank = T.rank_of(core)
     queues = {"g": g, "pe": g.tensor, "dve": g.vector, "sy": g.sync, "sc": g.scalar}
     seen, sent = {}, [0]
-    blocks = range(NCH)
 
-    def engines(src, dst):
-        return bin(topo.mask(cores[src], cores[dst])).count("1")
+    def pop(m):
+        return bin(m).count("1")
+
+    def eng(src, dst):
+        return pop(topo.mask(cores[src], cores[dst]))
 
     def wait(qn, s, v):
         if seen.get((qn, s), 0) < v:
@@ -49,204 +46,256 @@ def rank_program(g, core, T, topo):
     def load(qn, out, in_, s):
         queues[qn].dma_start(out, in_).then_inc(sem[s], 16)
 
-    def send(dst, out, in_, s):
-        rid, pid = topo.addr(cores[dst], core)
+    def put(dst_core, out, in_, s, mask=None):
+        m = topo.mask(core, dst_core) if mask is None else mask
+        rid, pid = topo.addr(dst_core, core)
         g.remote_dma(out_ap=out, in_ap=in_, remote_sem=sem[s], local_sem=sem.sent, pid=pid, routing_id=rid,
-                     dma_engine_mask=topo.mask(core, cores[dst]))
-        sent[0] += engines(rank, dst)
+                     dma_engine_mask=m)
+        sent[0] += pop(m)
 
-    def blk(buf, c):
-        return buf[:, c * CW:(c + 1) * CW]
+    def send(dst, out, in_, s):
+        put(cores[dst], out, in_, s)
 
-    def done(node, c):
-        return ("v_%s%d" % (node, c), 1)
+    def hb(buf, k):
+        return buf[:, k * CW:(k + 1) * CW]
 
-    def mm(node, pair, c, lhsT, rhs, start, stop, deps):
+    def ps(node):
+        return T["ps%d" % BANK[node]][:, 0:CW]
+
+    def mm(node, lhsT, rhs, start, stop, deps):
         for s, v in deps:
             wait("pe", s, v)
-        ins = g.tensor.matmul(T["ps%d" % (pair * NCH + c)][:, 0:CW], lhsT, blk(rhs, c), start, stop)
+        ins = g.tensor.matmul(ps(node), lhsT, rhs, start, stop)
         if stop:
-            ins.then_inc(sem["p_%s%d" % (node, c)], 1)
+            ins.then_inc(sem["p_" + node], 1)
 
-    def relu(node, pair, c, out):
+    def relu(node, out):
         wait("dve", "z", 1)
-        wait("dve", "p_%s%d" % (node, c), 1)
-        g.vector.tensor_tensor(blk(out, c), T["ps%d" % (pair * NCH + c)][:, 0:CW], T.zeros[:, 0:CW],
-                               AluOpType.max).then_inc(sem["v_%s%d" % (node, c)], 1)
+        wait("dve", "p_" + node, 1)
+        g.vector.tensor_tensor(out, ps(node), T.zeros[:], AluOpType.max).then_inc(sem["v_" + node], 1)
 
-    def store(buf):
-        g.sync.dma_start(T.y[:], buf[:]).then_inc(sem.st, 16)
-        g.sync.wait_ge(sem.st, 16)
+    def store(qn, k, src, deps):
+        for s, v in deps:
+            wait(qn, s, v)
+        queues[qn].dma_start(hb(T.y, k), src).then_inc(sem["st%d" % k], 16)
+        queues[qn].wait_ge(sem["st%d" % k], 16)
 
-    mine = [r for r in range(len(cores)) if topo.host(cores[r]) == topo.host(core)]
+    bases = sorted({min(r for r in range(n) if topo.host(cores[r]) == topo.host(c)) for c in cores})
+    half = n // 2
+    top, low = bases[0], bases[len(bases) // 2]
+
+    def rackmate(b):
+        return [x for x in bases if x != b and x // half == b // half][0]
+
+    def cabled(b):
+        return [x for x in bases if x // half != b // half and topo.may_write(cores[b], cores[x])][0]
+
+    near = cabled(top)
+    far = rackmate(near)
+    W8, W2, W3 = (0, 256), (256, 512), (512, 768)
+
+    jobs = [(top, W2, [rackmate(top), rackmate(top) + 1, top + 1], "r_w2t", "ld_wt"),
+            (low, W2, [rackmate(low), rackmate(low) + 1, low + 1], "r_w2t", "ld_wt"),
+            (top, W3, [near + 1, rackmate(top), rackmate(top) + 1, top + 1], "r_w3", "ld_wt"),
+            (low, W8, [rackmate(low), rackmate(low) + 1, low + 1], "r_w8", "ld_w8")]
+    plan = []
+    for R, cols, dests, s, ld in jobs:
+        c0 = cores[R]
+        taken = [p[1] for p in plan]
+        free = [c for c in range(max(0, c0 - topo.CORES_PER_CHIP), c0 + topo.CORES_PER_CHIP)
+                if topo.host(c) == topo.host(c0) and topo.chip(c) == topo.chip(c0) and topo.die(c) != topo.die(c0)
+                and all(topo.may_write(c, cores[d]) for d in dests) and c not in taken]
+        plan.append((R, free[0], cols, dests, s, ld))
+
+    def side(R, cc):
+        return topo.mask(cores[R], cc) & ~topo.mask(cores[R], cores[R + 1])
+
+    for R, cc, cols, dests, s, ld in plan:
+        if core == cc:
+            tile = T.wt[:, cols[0]:cols[1]]
+            wait("g", "r_c", pop(side(R, cc)))
+            for d in dests:
+                send(d, tile, tile, s)
+            wait("g", "sent", sent[0])
+            return
+    if rank is None:
+        return
+
+    mine = [r for r in range(n) if topo.host(cores[r]) == topo.host(core)]
     q, role = mine[0], mine.index(rank)
-    centres = sorted({min(r for r in range(len(cores)) if topo.host(cores[r]) == topo.host(c)) for c in cores})
+    A, B, L2, L3 = mine
 
-    if role != 0:
-        if role == 2:
-            load("sy", T.wus[:, 0:256], T.wu[:, 0:256], "ld_w")
-            wait("g", "ld_w", 16)
-            send(q, T.w2[:], T.wus[:, 0:256], "r_w2")
-        else:
-            g.vector.memset(T.zeros[:], 0.0).then_inc(sem.z, 1)
-        for c in blocks:
-            load("sc" if (role == 2 or c) else "sy", blk(T.xs, c), blk(T.x, c), "ld_x%d" % c)
-            wait("g", "ld_x%d" % c, 16)
-            send(q, blk(T["x%d" % role], c), blk(T.xs, c), "r_x%d_%d" % (role, c))
+    if role == 2:
+        load("sy", T.wus[:, 0:256], T.wu[:, 0:256], "ld_w0")
+        for k in (0, 1):
+            load("sc", hb(T.xs, k), hb(T.x, k), "ld_x%d" % k)
+        wait("g", "ld_w0", 16)
+        for c in (A, B):
+            send(c, T.v2[:], T.wus[:, 128:256], "r_v2")
+        for k in (0, 1):
+            mm("q%d" % k, T.wus[:, 0:128], hb(T.xs, k), True, True, [("ld_w0", 16), ("ld_x%d" % k, 16)])
+            wait("dve", "p_q%d" % k, 1)
+            g.vector.tensor_copy(hb(T.p2, k), ps("q%d" % k)).then_inc(sem["v_q%d" % k], 1)
+            wait("g", "v_q%d" % k, 1)
+            send(mine[k], T.x2[:], hb(T.p2, k), "r_x2")
         wait("sc", "sent", sent[0])
-        load("sc", T.wds[:], T.wd[:], "ld_d")
-        if role == 2:
-            wait("g", "ld_d", 16)
-            send(q, T.d2[:], T.wds[:], "r_d2")
-            wait("sy", "r_land", engines(q, rank))
-            store(T.yl)
-        else:
-            for c in blocks:
-                mm("lf", 0, c, T.wds[:, 0:128], T.xs, True, False, [("ld_d", 16), ("ld_x%d" % c, 16)])
-            for c in blocks:
-                mm("lf", 0, c, T.wds[:, 128:256], T.land, False, True,
-                   [("r_ln%d" % c if role == 1 else "r_land", engines(q, rank))])
-                relu("lf", 0, c, T.yo)
-                wait("sy", *done("lf", c))
-            store(T.yo)
+        load("sc", T.wdo[:], T.wd[:], "ld_o")
+        wait("g", "ld_o", 16)
+        for c in (A, B):
+            send(c, T.d2[:], T.wdo[:], "r_d2")
+        for k, qn in ((0, "sy"), (1, "sc")):
+            store(qn, k, hb(T.land, k), [("r_ln%d" % k, eng(mine[k], rank))])
         wait("g", "sent", sent[0])
         return
 
-    top, low = centres[0], centres[len(centres) // 2]
-    half = len(cores) // 2
+    if role == 3:
+        g.vector.memset(T.zeros[:], 0.0).then_inc(sem.z, 1)
+        for k, qn in ((0, "sy"), (1, "sc")):
+            load(qn, hb(T.xs, k), hb(T.x, k), "ld_x%d" % k)
+        for k in (0, 1):
+            wait("g", "ld_x%d" % k, 16)
+            send(mine[k], T.x3[:], hb(T.xs, k), "r_x3")
+        wait("sc", "sent", sent[0])
+        load("sc", T.wdo[:], T.wd[:], "ld_o")
+        for k in (0, 1):
+            mm("lf%d" % k, T.wdo[:, 0:128], hb(T.xs, k), True, False, [("ld_o", 16), ("ld_x%d" % k, 16)])
+        for k, qn in ((0, "sy"), (1, "sc")):
+            mm("lf%d" % k, T.wdo[:, 128:256], hb(T.land, k), False, True, [("r_ln%d" % k, eng(mine[k], rank))])
+            relu("lf%d" % k, hb(T.yo, k))
+            store(qn, k, hb(T.yo, k), [("v_lf%d" % k, 1)])
+        wait("g", "sent", sent[0])
+        return
+
+    k = role
+    other = mine[1 - k]
+    partner, cable = rackmate(q) + k, cabled(q) + k
     pair_root = q - q % half
-    partner = [c for c in centres if c != q and c // half == q // half][0]
-    cable = [c for c in centres if c // half != q // half and topo.may_write(core, cores[c])][0]
-    far = [c for c in centres if c != top and not topo.may_write(cores[top], cores[c])]
-    near = [c for c in centres if c != top and c not in far]
-    D8, E8, U3 = T.wt[:, 0:128], T.wt[:, 128:256], T.wt[:, 256:384]
-    U2, V2, V3 = T.wt[:, 384:512], T.wt[:, 512:640], T.wt[:, 640:768]
     in_low = pair_root == low
     own_node = q != pair_root
     sqn = "sq" if own_node else ("s8" if in_low else "rt")
+    D8, E8 = T.wt[:, 0:128], T.wt[:, 128:256]
+    U2, V2 = T.wt[:, 256:384], T.wt[:, 384:512]
+    U3, V3 = T.wt[:, 512:640], T.wt[:, 640:768]
+    w3 = T.wt[:, W3[0]:W3[1]]
 
     g.vector.memset(T.zeros[:], 0.0).then_inc(sem.z, 1)
-    if q == top:
-        load("sy", U3, T.wu[:, 768:896], "ld_u3")
-        load("sc", V3, T.wu[:, 896:1024], "ld_v3")
-        load("sy", T.wt[:, 384:640], T.wu[:, 512:768], "ld_wt")
-        load("sc", T.wus[:], T.wu[:, 0:512], "ld_w")
-        load("sy", T.xs[:], T.x[:], "ld_x")
-    elif q == low:
-        load("sy", T.wt[:, 384:640], T.wu[:, 512:768], "ld_wt")
-        load("sy", T.xs[:], T.x[:], "ld_x")
-        wait("sc", "ld_wt", 16)
-        load("sc", T.wus[:], T.wu[:, 0:512], "ld_w")
-        load("sc", T.wt[:, 0:256], T.wd[:], "ld_d")
+    if k == 0:
+        load("sc", T.wus[:, 0:256], T.wu[:, 0:256], "ld_w0")
+        load("sc", T.xs[:], T.x[:], "ld_x")
+        if rank == top:
+            load("sy", T.wt[:, 256:768], T.wu[:, 512:1024], "ld_wt")
+        elif rank == low:
+            load("sy", T.wt[:, 256:512], T.wu[:, 512:768], "ld_wt")
+            load("sy", T.wt[:, 0:256], T.wd[:], "ld_w8")
+        load("sy", T.wus[:, 256:512], T.wu[:, 256:512], "ld_w1")
+        if own_node:
+            load("sy", T.wds[:], T.wd[:], "ld_d")
     else:
         load("sy", T.xs[:], T.x[:], "ld_x")
-        load("sc", T.wus[:], T.wu[:, 0:512], "ld_w")
-        load("sy", T.wds[:], T.wd[:], "ld_d")
+        load("sc", T.wdo[:], T.wd[:], "ld_o")
 
-    have8 = []
-    if q == top:
-        have2, have3 = [("ld_wt", 16)], [("ld_u3", 16), ("ld_v3", 16)]
-    elif q == low:
-        have2, have8 = [("ld_wt", 16)], [("ld_d", 16)]
-        have3 = [("r_wa", sum(engines(n, q) for n in near))]
-    else:
-        have3 = [("r_wa", engines(top, q)), ("r_wb", engines(top, q))]
-        have2 = [("r_wb", engines(top, q))]
-        if in_low:
-            have2, have8 = [("r_wd", engines(low, q))], [("r_wc", engines(low, q))]
+    def via(s):
+        for R, cc, cols, dests, sm, ld in plan:
+            if sm == s and rank in dests:
+                return [(s, pop(topo.mask(cc, core)))]
+        return None
 
-    if q == top:
-        wait("g", "ld_u3", 16)
-        send(partner, U3, U3, "r_wa")
-        wait("g", "ld_v3", 16)
-        send(cable, V3, V3, "r_wa")
-        send(cable, U3, U3, "r_wb")
-        wait("g", "r_w2", engines(mine[2], q))
-        wait("g", "ld_wt", 16)
-        send(partner, T.wt[:, 384:768], T.wt[:, 384:768], "r_wb")
-    elif q == low:
-        wait("g", "ld_wt", 16)
-        send(partner, T.wt[:, 384:640], T.wt[:, 384:640], "r_wd")
+    have_w0 = [("ld_w0", 16)] if k == 0 else [("r_w0", eng(A, rank))]
+    have_w1 = [("ld_w1", 16)] if k == 0 else [("r_w1", eng(A, rank))]
+    have2 = [("ld_wt", 16)] if rank == pair_root else via("r_w2t")
+    if rank == top:
+        have3 = [("ld_wt", 16)]
+    elif via("r_w3"):
+        have3 = via("r_w3")
+    elif q == near:
+        have3 = [("r_w3", eng(top, rank))]
     else:
-        wait("g", "r_wa", engines(top, q))
-        tile = V3 if in_low else U3
-        for f in far:
-            send(f, tile, tile, "r_wa")
-    for c in blocks:
-        wait("g", *done("h", c))
-        send(partner, blk(T.hp, c), blk(T.h, c), "r_hp%d" % c)
-    if q == low:
+        have3 = [("r_w3", eng(near + k, rank))]
+    have8 = ([("ld_w8", 16)] if rank == low else via("r_w8")) if in_low else []
+    haved = [("ld_d", 16)] if k == 0 else [("r_wds", eng(A, rank))]
+
+    if k == 0:
+        wait("g", "ld_w0", 16)
+        send(B, T.wus[:, 0:256], T.wus[:, 0:256], "r_w0")
+        for R, cc, cols, dests, s, ld in plan:
+            if R == rank:
+                wait("g", ld, 16)
+                put(cc, T.wt[:, cols[0]:cols[1]], T.wt[:, cols[0]:cols[1]], "r_c", side(R, cc))
+        wait("g", "ld_x", 16)
+        send(B, T.xo[:], hb(T.xs, 1), "r_xo")
+        wait("g", "ld_w1", 16)
+        send(B, T.wus[:, 256:512], T.wus[:, 256:512], "r_w1")
+        if rank == top:
+            send(near, w3, w3, "r_w3")
+    else:
+        wait("g", "ld_x", 16)
+        send(A, T.xo[:], hb(T.xs, 0), "r_xo")
+    wait("g", "v_h", 1)
+    send(partner, T.hp[:], T.h[:], "r_hp")
+    if q == near:
+        for s, v in have3:
+            wait("g", s, v)
+        send(far + k, w3, w3, "r_w3")
+    if k == 0 and own_node:
         wait("g", "ld_d", 16)
-        send(partner, T.wt[:, 0:256], T.wt[:, 0:256], "r_wc")
-    for c in blocks:
-        wait("g", *done("ar", c))
-        send(cable, blk(T.ao, c), blk(T.ar, c), "r_ao%d" % c)
-    for c in blocks:
-        wait("g", *done(sqn, c))
-        send(mine[1], blk(T.land, c), blk(T[sqn], c), "r_ln%d" % c)
-    for c in blocks:
-        wait("g", *done("sp", c))
-    send(mine[3], T.land[:], T.sp[:], "r_land")
-    send(mine[2], T.yl[:], T.sp[:], "r_land")
+        send(B, T.wds[:], T.wds[:], "r_wds")
+    wait("g", "v_ar", 1)
+    send(cable, T.ao[:], T.ar[:], "r_ao")
+    wait("g", "v_" + sqn, 1)
+    send(other, hb(T.land, k), T[sqn][:], "r_land")
+    wait("g", "v_sp", 1)
+    send(L3, hb(T.land, k), T.sp[:], "r_ln%d" % k)
+    send(L2, hb(T.land, k), T.sp[:], "r_ln%d" % k)
     wait("g", "sent", sent[0])
 
-    def came(leaf, c):
-        return ("r_x%d_%d" % (leaf, c), engines(mine[leaf], q))
+    U0, V0, U1, V1 = (T.wus[:, 128 * i:128 * (i + 1)] for i in range(4))
+    mm("a", V0 if k else U0, hb(T.xs, k), True, False, have_w0 + [("ld_x", 16)])
+    mm("a", U0 if k else V0, T.xo[:], False, True, [("r_xo", eng(other, rank))])
+    relu("a", T.a[:])
+    mm("s2", T.v2[:], T.x3[:], True, True, [("r_v2", eng(L2, rank)), ("r_x3", eng(L3, rank))])
+    wait("dve", "p_s2", 1)
+    wait("dve", "r_x2", eng(L2, rank))
+    g.vector.tensor_tensor(ps("s2"), ps("s2"), T.x2[:], AluOpType.add).then_inc(sem.t_s2, 1)
+    wait("dve", "t_s2", 1)
+    g.vector.tensor_tensor(T.s2[:], ps("s2"), T.zeros[:], AluOpType.max).then_inc(sem.v_s2, 1)
+    mm("h", U1, T.a[:], True, False, have_w1 + [("v_a", 1)])
+    mm("h", V1, T.s2[:], False, True, [("v_s2", 1)])
+    relu("h", T.h[:])
 
-    def a_fin(c):
-        mm("a", 0, c, T.wus[:, 128:256], T.x1, False, True, [came(1, c)])
-        relu("a", 0, c, T.a)
+    mm("ar", V2 if own_node else U2, T.h[:], True, False, have2 + [("v_h", 1)])
+    mm("ar", U2 if own_node else V2, T.hp[:], False, True, [("r_hp", eng(partner, rank))])
+    relu("ar", T.ar[:])
 
-    def s2_pre(c):
-        mm("s2", 1, c, T.w2[:, 128:256], T.x3, True, False, [("r_w2", engines(mine[2], q)), came(3, c)])
-
-    def s2_fin(c):
-        mm("s2", 1, c, T.w2[:, 0:128], T.x2, False, True, [came(2, c)])
-        relu("s2", 1, c, T.s2)
-
-    def h_pre(c):
-        mm("h", 2, c, T.wus[:, 256:384], T.a, True, False, [done("a", c)])
-
-    def h_fin(c):
-        mm("h", 2, c, T.wus[:, 384:512], T.s2, False, True, [done("s2", c)])
-        relu("h", 2, c, T.h)
-
-    for c in blocks:
-        mm("a", 0, c, T.wus[:, 0:128], T.xs, True, False, [("ld_w", 16), ("ld_x", 16)])
-    a_fin(0), s2_pre(0), h_pre(0), s2_fin(0), a_fin(1), s2_pre(1), h_fin(0), h_pre(1), s2_fin(1), h_fin(1)
-
-    for c in blocks:
-        if own_node:
-            mm("sq", 0, c, T.wds[:, 0:128], T.h, True, False, [("ld_d", 16), done("h", c)])
-        mm("ar", 3, c, V2 if own_node else U2, T.h, True, False, have2 + [done("h", c)])
-    for c in blocks:
-        mm("ar", 3, c, U2 if own_node else V2, T.hp, False, True, [("r_hp%d" % c, engines(partner, q))])
-        relu("ar", 3, c, T.ar)
-    for c in blocks:
-        mm("rt", 2, c, V3 if in_low else U3, T.ar, True, False, have3 + [done("ar", c)])
-        if in_low:
-            mm("s8", 3, c, D8, T.ar, True, False, have8 + [done("ar", c)])
-        mm("sp", 1, c, T.d2[:, 0:128], T.s2, True, False, [("r_d2", engines(mine[2], q)), done("s2", c)])
-
-    chain = [("rt", 2, U3 if in_low else V3, T.ao, None)]
+    mm("rt", V3 if in_low else U3, T.ar[:], True, False, have3 + [("v_ar", 1)])
     if in_low:
-        chain.append(("s8", 3, E8, T.rt, "rt"))
+        mm("s8", D8, T.ar[:], True, False, have8)
     if own_node:
-        chain.append(("sq", 0, T.wds[:, 128:256], T[chain[-1][0]], chain[-1][0]))
-    chain.append(("sp", 1, T.d2[:, 128:256], T[sqn], sqn))
-    order, nxt = [(0, 0), (1, 0)], [2, 0]
-    while nxt[0] < len(chain) or nxt[1] < len(chain):
-        for c in (1, 0):
-            if nxt[c] < len(chain):
-                order.append((nxt[c], c))
-                nxt[c] += 1
-    for k, c in order:
-        node, pair, tile, operand, src = chain[k]
-        mm(node, pair, c, tile, operand, False, True,
-           [done(src, c)] if src else [("r_ao%d" % c, engines(cable, q))])
-        relu(node, pair, c, T[node])
+        mm("sq", T.wds[:, 0:128], T.h[:], True, False, haved)
+    mm("sp", T.d2[:, 0:128], T.s2[:], True, False, [("r_d2", eng(L2, rank))])
+    if k == 1:
+        for c in (0, 1):
+            mm("lf%d" % c, T.wdo[:, 0:128], hb(T.xs, c), True, False, [("ld_o", 16)])
 
-    for c in blocks:
-        wait("sy", *done(sqn, c))
-    wait("sy", "sent", sent[0])
-    store(T[sqn])
+    mm("rt", U3 if in_low else V3, T.ao[:], False, True, [("r_ao", eng(cable, rank))])
+    relu("rt", T.rt[:])
+    last = "rt"
+    if in_low:
+        mm("s8", E8, T.rt[:], False, True, [("v_rt", 1)])
+        relu("s8", T.s8[:])
+        last = "s8"
+    if own_node:
+        mm("sq", T.wds[:, 128:256], T[last][:], False, True, [("v_" + last, 1)])
+        relu("sq", T.sq[:])
+    mm("sp", T.d2[:, 128:256], T[sqn][:], False, True, [("v_" + sqn, 1)])
+    relu("sp", T.sp[:])
+
+    if k == 0:
+        store("sc", 1, hb(T.land, 1), [("r_land", eng(B, rank))])
+        store("sy", 0, T[sqn][:], [("v_" + sqn, 1), ("sent", sent[0])])
+    else:
+        mm("lf1", T.wdo[:, 128:256], T[sqn][:], False, True, [])
+        relu("lf1", hb(T.yo, 1))
+        mm("lf0", T.wdo[:, 128:256], hb(T.land, 0), False, True, [("r_land", eng(A, rank))])
+        relu("lf0", hb(T.yo, 0))
+        store("sc", 0, hb(T.yo, 0), [("v_lf0", 1)])
+        store("sy", 1, hb(T.yo, 1), [("v_lf1", 1), ("sent", sent[0])])

@@ -2,7 +2,10 @@ from concourse.mybir import AluOpType
 
 TK = 512
 CW = TK // 2
-BANK = {"a": 0, "s2": 1, "h": 2, "ar": 3, "rt": 4, "s8": 5, "sq": 6, "sp": 7, "lf0": 0, "lf1": 1, "q0": 0, "q1": 1}
+NB = 2
+SW = CW // NB
+BANK = {"a": 0, "s2": 2, "h": 4, "ar": 6, "rt": 0, "s8": 2, "sq": 4, "sp": 6, "lf1": 0, "lf0": 2, "q0": 0, "q1": 1,
+        "p0": 6}
 
 
 def _bf(cols):
@@ -13,16 +16,19 @@ SCRATCH = {
     "xs": _bf(TK), "wus": _bf(512), "wds": _bf(256), "wdo": _bf(256), "zeros": ("sbuf", [128, CW], "float32"),
     "xo": _bf(CW), "x2": _bf(CW), "x3": _bf(CW), "v2": _bf(128), "d2": _bf(256), "wt": _bf(768),
     "hp": _bf(CW), "ao": _bf(CW), "a": _bf(CW), "s2": _bf(CW), "h": _bf(CW), "ar": _bf(CW), "rt": _bf(CW),
-    "s8": _bf(CW), "sq": _bf(CW), "sp": _bf(CW), "land": _bf(TK), "yo": _bf(TK), "p2": _bf(TK),
+    "s8": _bf(CW), "sq": _bf(CW), "sp": _bf(CW), "land": _bf(TK), "yo": _bf(TK), "p2": _bf(TK), "p0": _bf(CW),
 }
 for _i in range(8):
     SCRATCH["ps%d" % _i] = ("psum", [128, 512], "float32")
 
 SEMAPHORES = ["ld_x", "ld_x0", "ld_x1", "ld_w0", "ld_w1", "ld_wt", "ld_w8", "ld_d", "ld_o", "z", "sent", "st0", "st1",
-              "r_c", "r_w0", "r_w1", "r_xo", "r_v2", "r_x2", "r_x3", "r_d2", "r_w2t", "r_w3", "r_w8", "r_wds",
-              "r_hp", "r_ao", "r_land", "r_ln0", "r_ln1", "t_s2"]
+              "r_c", "r_w0", "r_w1", "r_v2", "r_d2", "r_w2t", "r_w3", "r_w8", "r_wds"]
 for _n in BANK:
-    SEMAPHORES += ["p_" + _n, "v_" + _n]
+    for _c in range(NB):
+        SEMAPHORES += ["p_%s%d" % (_n, _c), "v_%s%d" % (_n, _c)]
+for _c in range(NB):
+    SEMAPHORES += ["%s%d" % (_n, _c) for _n in ("t_a", "t_s2", "r_xo", "r_x2", "r_x3", "r_hp", "r_ao", "r_land",
+                                                "r_ln0", "r_ln1")]
 
 
 def rank_program(g, core, T, topo):
@@ -31,6 +37,7 @@ def rank_program(g, core, T, topo):
     rank = T.rank_of(core)
     queues = {"g": g, "pe": g.tensor, "dve": g.vector, "sy": g.sync, "sc": g.scalar}
     seen, sent = {}, [0]
+    subs = range(NB)
 
     def pop(m):
         return bin(m).count("1")
@@ -59,20 +66,36 @@ def rank_program(g, core, T, topo):
     def hb(buf, k):
         return buf[:, k * CW:(k + 1) * CW]
 
-    def ps(node):
-        return T["ps%d" % BANK[node]][:, 0:CW]
+    def sb(buf, c, off=0):
+        return buf[:, off + c * SW:off + (c + 1) * SW]
 
-    def mm(node, lhsT, rhs, start, stop, deps):
+    def ps(node, c):
+        return T["ps%d" % (BANK[node] + c)][:, 0:SW]
+
+    def done(node):
+        return [("v_%s%d" % (node, c), 1) for c in subs]
+
+    def mm(node, c, lhsT, rhs, off, start, stop, deps):
         for s, v in deps:
             wait("pe", s, v)
-        ins = g.tensor.matmul(ps(node), lhsT, rhs, start, stop)
+        ins = g.tensor.matmul(ps(node, c), lhsT, sb(rhs, c, off), start, stop)
         if stop:
-            ins.then_inc(sem["p_" + node], 1)
+            ins.then_inc(sem["p_%s%d" % (node, c)], 1)
 
-    def relu(node, out):
+    def relu(node, c, out, off=0):
         wait("dve", "z", 1)
-        wait("dve", "p_" + node, 1)
-        g.vector.tensor_tensor(out, ps(node), T.zeros[:], AluOpType.max).then_inc(sem["v_" + node], 1)
+        wait("dve", "p_%s%d" % (node, c), 1)
+        g.vector.tensor_tensor(sb(out, c, off), ps(node, c), T.zeros[:, 0:SW],
+                               AluOpType.max).then_inc(sem["v_%s%d" % (node, c)], 1)
+
+    def addrelu(node, c, part, deps, out):
+        for s, v in [("z", 1), ("p_%s%d" % (node, c), 1)] + deps:
+            wait("dve", s, v)
+        g.vector.tensor_tensor(ps(node, c), ps(node, c), sb(part, c), AluOpType.add).then_inc(
+            sem["t_%s%d" % (node, c)], 1)
+        wait("dve", "t_%s%d" % (node, c), 1)
+        g.vector.tensor_tensor(sb(out, c), ps(node, c), T.zeros[:, 0:SW],
+                               AluOpType.max).then_inc(sem["v_%s%d" % (node, c)], 1)
 
     def store(qn, k, src, deps):
         for s, v in deps:
@@ -133,18 +156,23 @@ def rank_program(g, core, T, topo):
         for c in (A, B):
             send(c, T.v2[:], T.wus[:, 128:256], "r_v2")
         for k in (0, 1):
-            mm("q%d" % k, T.wus[:, 0:128], hb(T.xs, k), True, True, [("ld_w0", 16), ("ld_x%d" % k, 16)])
-            wait("dve", "p_q%d" % k, 1)
-            g.vector.tensor_copy(hb(T.p2, k), ps("q%d" % k)).then_inc(sem["v_q%d" % k], 1)
-            wait("g", "v_q%d" % k, 1)
-            send(mine[k], T.x2[:], hb(T.p2, k), "r_x2")
+            wait("pe", "ld_w0", 16)
+            wait("pe", "ld_x%d" % k, 16)
+            bank = T["ps%d" % BANK["q%d" % k]][:, 0:CW]
+            g.tensor.matmul(bank, T.wus[:, 0:128], hb(T.xs, k), True, True).then_inc(sem["p_q%d0" % k], 1)
+            wait("dve", "p_q%d0" % k, 1)
+            g.vector.tensor_copy(hb(T.p2, k), bank).then_inc(sem["v_q%d0" % k], 1)
+        for c in subs:
+            for k in (0, 1):
+                wait("g", "v_q%d0" % k, 1)
+                send(mine[k], sb(T.x2, c), sb(T.p2, c, k * CW), "r_x2%d" % c)
         wait("sc", "sent", sent[0])
         load("sc", T.wdo[:], T.wd[:], "ld_o")
         wait("g", "ld_o", 16)
         for c in (A, B):
             send(c, T.d2[:], T.wdo[:], "r_d2")
         for k, qn in ((0, "sy"), (1, "sc")):
-            store(qn, k, hb(T.land, k), [("r_ln%d" % k, eng(mine[k], rank))])
+            store(qn, k, hb(T.land, k), [("r_ln%d%d" % (k, c), eng(mine[k], rank)) for c in subs])
         wait("g", "sent", sent[0])
         return
 
@@ -152,17 +180,22 @@ def rank_program(g, core, T, topo):
         g.vector.memset(T.zeros[:], 0.0).then_inc(sem.z, 1)
         for k, qn in ((0, "sy"), (1, "sc")):
             load(qn, hb(T.xs, k), hb(T.x, k), "ld_x%d" % k)
-        for k in (0, 1):
-            wait("g", "ld_x%d" % k, 16)
-            send(mine[k], T.x3[:], hb(T.xs, k), "r_x3")
+        for c in subs:
+            for k in (0, 1):
+                wait("g", "ld_x%d" % k, 16)
+                send(mine[k], sb(T.x3, c), sb(T.xs, c, k * CW), "r_x3%d" % c)
         wait("sc", "sent", sent[0])
         load("sc", T.wdo[:], T.wd[:], "ld_o")
-        for k in (0, 1):
-            mm("lf%d" % k, T.wdo[:, 0:128], hb(T.xs, k), True, False, [("ld_o", 16), ("ld_x%d" % k, 16)])
+        for c in subs:
+            for k in (0, 1):
+                mm("lf%d" % k, c, T.wdo[:, 0:128], T.xs, k * CW, True, False, [("ld_o", 16), ("ld_x%d" % k, 16)])
+        for c in subs:
+            for k in (0, 1):
+                mm("lf%d" % k, c, T.wdo[:, 128:256], T.land, k * CW, False, True,
+                   [("r_ln%d%d" % (k, c), eng(mine[k], rank))])
+                relu("lf%d" % k, c, T.yo, k * CW)
         for k, qn in ((0, "sy"), (1, "sc")):
-            mm("lf%d" % k, T.wdo[:, 128:256], hb(T.land, k), False, True, [("r_ln%d" % k, eng(mine[k], rank))])
-            relu("lf%d" % k, hb(T.yo, k))
-            store(qn, k, hb(T.yo, k), [("v_lf%d" % k, 1)])
+            store(qn, k, hb(T.yo, k), done("lf%d" % k))
         wait("g", "sent", sent[0])
         return
 
@@ -214,88 +247,111 @@ def rank_program(g, core, T, topo):
     have8 = ([("ld_w8", 16)] if rank == low else via("r_w8")) if in_low else []
     haved = [("ld_d", 16)] if k == 0 else [("r_wds", eng(A, rank))]
 
+    def v(node, c):
+        return ("v_%s%d" % (node, c), 1)
+
+    U0, V0, U1, V1 = (T.wus[:, 128 * i:128 * (i + 1)] for i in range(4))
     if k == 0:
         wait("g", "ld_w0", 16)
-        send(B, T.wus[:, 0:256], T.wus[:, 0:256], "r_w0")
+        send(B, V0, V0, "r_w0")
         for R, cc, cols, dests, s, ld in plan:
             if R == rank:
                 wait("g", ld, 16)
                 put(cc, T.wt[:, cols[0]:cols[1]], T.wt[:, cols[0]:cols[1]], "r_c", side(R, cc))
-        wait("g", "ld_x", 16)
-        send(B, T.xo[:], hb(T.xs, 1), "r_xo")
+        wait("g", *v("p0", 0))
+        send(B, sb(T.xo, 0), sb(T.p0, 0), "r_xo0")
         wait("g", "ld_w1", 16)
         send(B, T.wus[:, 256:512], T.wus[:, 256:512], "r_w1")
+        wait("g", *v("p0", 1))
+        send(B, sb(T.xo, 1), sb(T.p0, 1), "r_xo1")
         if rank == top:
             send(near, w3, w3, "r_w3")
     else:
         wait("g", "ld_x", 16)
-        send(A, T.xo[:], hb(T.xs, 0), "r_xo")
-    wait("g", "v_h", 1)
-    send(partner, T.hp[:], T.h[:], "r_hp")
+        send(A, T.xo[:], hb(T.xs, 0), "r_xo0")
+    for c in subs:
+        wait("g", *v("h", c))
+        send(partner, sb(T.hp, c), sb(T.h, c), "r_hp%d" % c)
     if q == near:
-        for s, v in have3:
-            wait("g", s, v)
+        for s, n_ in have3:
+            wait("g", s, n_)
         send(far + k, w3, w3, "r_w3")
     if k == 0 and own_node:
         wait("g", "ld_d", 16)
         send(B, T.wds[:], T.wds[:], "r_wds")
-    wait("g", "v_ar", 1)
-    send(cable, T.ao[:], T.ar[:], "r_ao")
-    wait("g", "v_" + sqn, 1)
-    send(other, hb(T.land, k), T[sqn][:], "r_land")
-    wait("g", "v_sp", 1)
-    send(L3, hb(T.land, k), T.sp[:], "r_ln%d" % k)
-    send(L2, hb(T.land, k), T.sp[:], "r_ln%d" % k)
+    for c in subs:
+        wait("g", *v("ar", c))
+        send(cable, sb(T.ao, c), sb(T.ar, c), "r_ao%d" % c)
+    for c in subs:
+        wait("g", *v(sqn, c))
+        send(other, sb(T.land, c, k * CW), sb(T[sqn], c), "r_land%d" % c)
+        wait("g", *v("sp", c))
+        send(L3, sb(T.land, c, k * CW), sb(T.sp, c), "r_ln%d%d" % (k, c))
+        send(L2, sb(T.land, c, k * CW), sb(T.sp, c), "r_ln%d%d" % (k, c))
     wait("g", "sent", sent[0])
 
-    U0, V0, U1, V1 = (T.wus[:, 128 * i:128 * (i + 1)] for i in range(4))
-    mm("a", V0 if k else U0, hb(T.xs, k), True, False, have_w0 + [("ld_x", 16)])
-    mm("a", U0 if k else V0, T.xo[:], False, True, [("r_xo", eng(other, rank))])
-    relu("a", T.a[:])
-    mm("s2", T.v2[:], T.x3[:], True, True, [("r_v2", eng(L2, rank)), ("r_x3", eng(L3, rank))])
-    wait("dve", "p_s2", 1)
-    wait("dve", "r_x2", eng(L2, rank))
-    g.vector.tensor_tensor(ps("s2"), ps("s2"), T.x2[:], AluOpType.add).then_inc(sem.t_s2, 1)
-    wait("dve", "t_s2", 1)
-    g.vector.tensor_tensor(T.s2[:], ps("s2"), T.zeros[:], AluOpType.max).then_inc(sem.v_s2, 1)
-    mm("h", U1, T.a[:], True, False, have_w1 + [("v_a", 1)])
-    mm("h", V1, T.s2[:], False, True, [("v_s2", 1)])
-    relu("h", T.h[:])
+    if k == 0:
+        for c in subs:
+            mm("p0", c, U0, T.xs, CW, True, True, have_w0 + [("ld_x", 16)])
+            wait("dve", "p_p0%d" % c, 1)
+            g.vector.tensor_copy(sb(T.p0, c), ps("p0", c)).then_inc(sem["v_p0%d" % c], 1)
+        for c in subs:
+            mm("a", c, U0, T.xs, 0, True, False, [])
+    for c in subs:
+        if k == 0:
+            mm("a", c, V0, T.xo, 0, False, True, [("r_xo0", eng(B, rank))])
+            relu("a", c, T.a)
+        else:
+            mm("a", c, V0, T.xs, CW, True, True, have_w0 + [("ld_x", 16)])
+            addrelu("a", c, T.xo, [("r_xo%d" % c, eng(A, rank))], T.a)
+        mm("s2", c, T.v2[:], T.x3, 0, True, True, [("r_v2", eng(L2, rank)), ("r_x3%d" % c, eng(L3, rank))])
+        addrelu("s2", c, T.x2, [("r_x2%d" % c, eng(L2, rank))], T.s2)
+        mm("h", c, U1, T.a, 0, True, False, have_w1 + [v("a", c)])
+        mm("h", c, V1, T.s2, 0, False, True, [v("s2", c)])
+        relu("h", c, T.h)
+    for c in subs:
+        mm("ar", c, V2 if own_node else U2, T.h, 0, True, False,
+           have2 + [v("h", c)] + ([v("p0", c)] if k == 0 else []))
+    for c in subs:
+        mm("ar", c, U2 if own_node else V2, T.hp, 0, False, True, [("r_hp%d" % c, eng(partner, rank))])
+        relu("ar", c, T.ar)
+    for c in subs:
+        mm("rt", c, V3 if in_low else U3, T.ar, 0, True, False, have3 + [v("ar", c)])
+        if in_low:
+            mm("s8", c, D8, T.ar, 0, True, False, have8)
+        if own_node:
+            mm("sq", c, T.wds[:, 0:128], T.h, 0, True, False, haved)
+        mm("sp", c, T.d2[:, 0:128], T.s2, 0, True, False, [("r_d2", eng(L2, rank))])
 
-    mm("ar", V2 if own_node else U2, T.h[:], True, False, have2 + [("v_h", 1)])
-    mm("ar", U2 if own_node else V2, T.hp[:], False, True, [("r_hp", eng(partner, rank))])
-    relu("ar", T.ar[:])
-
-    mm("rt", V3 if in_low else U3, T.ar[:], True, False, have3 + [("v_ar", 1)])
+    chain = [("rt", U3 if in_low else V3, T.ao, None)]
     if in_low:
-        mm("s8", D8, T.ar[:], True, False, have8)
+        chain.append(("s8", E8, T.rt, "rt"))
     if own_node:
-        mm("sq", T.wds[:, 0:128], T.h[:], True, False, haved)
-    mm("sp", T.d2[:, 0:128], T.s2[:], True, False, [("r_d2", eng(L2, rank))])
-    if k == 1:
-        for c in (0, 1):
-            mm("lf%d" % c, T.wdo[:, 0:128], hb(T.xs, c), True, False, [("ld_o", 16)])
-
-    mm("rt", U3 if in_low else V3, T.ao[:], False, True, [("r_ao", eng(cable, rank))])
-    relu("rt", T.rt[:])
-    last = "rt"
-    if in_low:
-        mm("s8", E8, T.rt[:], False, True, [("v_rt", 1)])
-        relu("s8", T.s8[:])
-        last = "s8"
-    if own_node:
-        mm("sq", T.wds[:, 128:256], T[last][:], False, True, [("v_" + last, 1)])
-        relu("sq", T.sq[:])
-    mm("sp", T.d2[:, 128:256], T[sqn][:], False, True, [("v_" + sqn, 1)])
-    relu("sp", T.sp[:])
+        chain.append(("sq", T.wds[:, 128:256], T[chain[-1][0]], chain[-1][0]))
+    chain.append(("sp", T.d2[:, 128:256], T[sqn], sqn))
+    order, nxt = [(0, 0), (1, 0)], [2, 0]
+    while nxt[0] < len(chain) or nxt[1] < len(chain):
+        for c in (1, 0):
+            if nxt[c] < len(chain):
+                order.append((nxt[c], c))
+                nxt[c] += 1
+    for i, c in order:
+        node, tile, operand, src = chain[i]
+        mm(node, c, tile, operand, 0, False, True, [v(src, c)] if src else [("r_ao%d" % c, eng(cable, rank))])
+        relu(node, c, T[node])
 
     if k == 0:
-        store("sc", 1, hb(T.land, 1), [("r_land", eng(B, rank))])
-        store("sy", 0, T[sqn][:], [("v_" + sqn, 1), ("sent", sent[0])])
+        store("sc", 1, hb(T.land, 1), [("r_land%d" % c, eng(B, rank)) for c in subs])
+        store("sy", 0, T[sqn][:], done(sqn) + [("sent", sent[0])])
     else:
-        mm("lf1", T.wdo[:, 128:256], T[sqn][:], False, True, [])
-        relu("lf1", hb(T.yo, 1))
-        mm("lf0", T.wdo[:, 128:256], hb(T.land, 0), False, True, [("r_land", eng(A, rank))])
-        relu("lf0", hb(T.yo, 0))
-        store("sc", 0, hb(T.yo, 0), [("v_lf0", 1)])
-        store("sy", 1, hb(T.yo, 1), [("v_lf1", 1), ("sent", sent[0])])
+        for c in subs:
+            mm("lf1", c, T.wdo[:, 0:128], T.xs, CW, True, False, [("ld_o", 16)])
+            mm("lf0", c, T.wdo[:, 0:128], T.xs, 0, True, False, [])
+        for c in subs:
+            mm("lf1", c, T.wdo[:, 128:256], T[sqn], 0, False, True, [])
+            relu("lf1", c, T.yo, CW)
+        for c in subs:
+            mm("lf0", c, T.wdo[:, 128:256], T.land, 0, False, True, [("r_land%d" % c, eng(A, rank))])
+            relu("lf0", c, T.yo, 0)
+        store("sc", 0, hb(T.yo, 0), done("lf0"))
+        store("sy", 1, hb(T.yo, 1), done("lf1") + [("sent", sent[0])])

from concourse.mybir import AluOpType

TK = 512
CW = TK // 2
NB = 2
SW = CW // NB
BANK = {"a": 0, "s2": 2, "h": 4, "ar": 6, "rt": 0, "s8": 2, "sq": 4, "sp": 6, "lf1": 0, "lf0": 2, "q0": 0, "q1": 1,
        "p0": 6}


def _bf(cols):
    return ("sbuf", [128, cols], "bfloat16")


SCRATCH = {
    "xs": _bf(TK), "wus": _bf(512), "wds": _bf(256), "wdo": _bf(256), "zeros": ("sbuf", [128, CW], "float32"),
    "xo": _bf(CW), "x2": _bf(CW), "x3": _bf(CW), "v2": _bf(128), "d2": _bf(256), "wt": _bf(768),
    "hp": _bf(CW), "ao": _bf(CW), "a": _bf(CW), "s2": _bf(CW), "h": _bf(CW), "ar": _bf(CW), "rt": _bf(CW),
    "s8": _bf(CW), "sq": _bf(CW), "sp": _bf(CW), "land": _bf(TK), "yo": _bf(TK), "p2": _bf(TK), "p0": _bf(CW),
}
for _i in range(8):
    SCRATCH["ps%d" % _i] = ("psum", [128, 512], "float32")

SEMAPHORES = ["ld_x", "ld_x0", "ld_x1", "ld_w0", "ld_w1", "ld_wt", "ld_w8", "ld_d", "ld_o", "z", "sent", "st0", "st1",
              "r_c", "r_w0", "r_w1", "r_v2", "r_d2", "r_w2t", "r_w3", "r_w8", "r_wds"]
for _n in BANK:
    for _c in range(NB):
        SEMAPHORES += ["p_%s%d" % (_n, _c), "v_%s%d" % (_n, _c)]
for _c in range(NB):
    SEMAPHORES += ["%s%d" % (_n, _c) for _n in ("t_a", "t_s2", "r_xo", "r_x2", "r_x3", "r_hp", "r_ao", "r_land",
                                                "r_ln0", "r_ln1")]


def rank_program(g, core, T, topo):
    cores, sem = T.cores, T.sem
    n = len(cores)
    rank = T.rank_of(core)
    queues = {"g": g, "pe": g.tensor, "dve": g.vector, "sy": g.sync, "sc": g.scalar}
    seen, sent = {}, [0]
    subs = range(NB)

    def pop(m):
        return bin(m).count("1")

    def eng(src, dst):
        return pop(topo.mask(cores[src], cores[dst]))

    def wait(qn, s, v):
        if seen.get((qn, s), 0) < v:
            seen[(qn, s)] = v
            queues[qn].wait_ge(sem[s], v)

    def load(qn, out, in_, s):
        queues[qn].dma_start(out, in_).then_inc(sem[s], 16)

    def put(dst_core, out, in_, s, mask=None):
        m = topo.mask(core, dst_core) if mask is None else mask
        rid, pid = topo.addr(dst_core, core)
        g.remote_dma(out_ap=out, in_ap=in_, remote_sem=sem[s], local_sem=sem.sent, pid=pid, routing_id=rid,
                     dma_engine_mask=m)
        sent[0] += pop(m)

    def send(dst, out, in_, s):
        put(cores[dst], out, in_, s)

    def hb(buf, k):
        return buf[:, k * CW:(k + 1) * CW]

    def sb(buf, c, off=0):
        return buf[:, off + c * SW:off + (c + 1) * SW]

    def ps(node, c):
        return T["ps%d" % (BANK[node] + c)][:, 0:SW]

    def done(node):
        return [("v_%s%d" % (node, c), 1) for c in subs]

    def mm(node, c, lhsT, rhs, off, start, stop, deps):
        for s, v in deps:
            wait("pe", s, v)
        ins = g.tensor.matmul(ps(node, c), lhsT, sb(rhs, c, off), start, stop)
        if stop:
            ins.then_inc(sem["p_%s%d" % (node, c)], 1)

    def relu(node, c, out, off=0):
        wait("dve", "z", 1)
        wait("dve", "p_%s%d" % (node, c), 1)
        g.vector.tensor_tensor(sb(out, c, off), ps(node, c), T.zeros[:, 0:SW],
                               AluOpType.max).then_inc(sem["v_%s%d" % (node, c)], 1)

    def addrelu(node, c, part, deps, out):
        for s, v in [("z", 1), ("p_%s%d" % (node, c), 1)] + deps:
            wait("dve", s, v)
        g.vector.tensor_tensor(ps(node, c), ps(node, c), sb(part, c), AluOpType.add).then_inc(
            sem["t_%s%d" % (node, c)], 1)
        wait("dve", "t_%s%d" % (node, c), 1)
        g.vector.tensor_tensor(sb(out, c), ps(node, c), T.zeros[:, 0:SW],
                               AluOpType.max).then_inc(sem["v_%s%d" % (node, c)], 1)

    def store(qn, k, src, deps):
        for s, v in deps:
            wait(qn, s, v)
        queues[qn].dma_start(hb(T.y, k), src).then_inc(sem["st%d" % k], 16)
        queues[qn].wait_ge(sem["st%d" % k], 16)

    bases = sorted({min(r for r in range(n) if topo.host(cores[r]) == topo.host(c)) for c in cores})
    half = n // 2
    top, low = bases[0], bases[len(bases) // 2]

    def rackmate(b):
        return [x for x in bases if x != b and x // half == b // half][0]

    def cabled(b):
        return [x for x in bases if x // half != b // half and topo.may_write(cores[b], cores[x])][0]

    near = cabled(top)
    far = rackmate(near)
    W8, W2, W3 = (0, 256), (256, 512), (512, 768)

    jobs = [(top, W2, [rackmate(top), rackmate(top) + 1, top + 1], "r_w2t", "ld_wt"),
            (low, W2, [rackmate(low), rackmate(low) + 1, low + 1], "r_w2t", "ld_wt"),
            (top, W3, [near + 1, rackmate(top), rackmate(top) + 1, top + 1], "r_w3", "ld_wt"),
            (low, W8, [rackmate(low), rackmate(low) + 1, low + 1], "r_w8", "ld_w8")]
    plan = []
    for R, cols, dests, s, ld in jobs:
        c0 = cores[R]
        taken = [p[1] for p in plan]
        free = [c for c in range(max(0, c0 - topo.CORES_PER_CHIP), c0 + topo.CORES_PER_CHIP)
                if topo.host(c) == topo.host(c0) and topo.chip(c) == topo.chip(c0) and topo.die(c) != topo.die(c0)
                and all(topo.may_write(c, cores[d]) for d in dests) and c not in taken]
        plan.append((R, free[0], cols, dests, s, ld))

    def side(R, cc):
        return topo.mask(cores[R], cc) & ~topo.mask(cores[R], cores[R + 1])

    for R, cc, cols, dests, s, ld in plan:
        if core == cc:
            tile = T.wt[:, cols[0]:cols[1]]
            wait("g", "r_c", pop(side(R, cc)))
            for d in dests:
                send(d, tile, tile, s)
            wait("g", "sent", sent[0])
            return
    if rank is None:
        return

    mine = [r for r in range(n) if topo.host(cores[r]) == topo.host(core)]
    q, role = mine[0], mine.index(rank)
    A, B, L2, L3 = mine

    if role == 2:
        load("sy", T.wus[:, 0:256], T.wu[:, 0:256], "ld_w0")
        for k in (0, 1):
            load("sc", hb(T.xs, k), hb(T.x, k), "ld_x%d" % k)
        wait("g", "ld_w0", 16)
        for c in (A, B):
            send(c, T.v2[:], T.wus[:, 128:256], "r_v2")
        for k in (0, 1):
            wait("pe", "ld_w0", 16)
            wait("pe", "ld_x%d" % k, 16)
            bank = T["ps%d" % BANK["q%d" % k]][:, 0:CW]
            g.tensor.matmul(bank, T.wus[:, 0:128], hb(T.xs, k), True, True).then_inc(sem["p_q%d0" % k], 1)
            wait("dve", "p_q%d0" % k, 1)
            g.vector.tensor_copy(hb(T.p2, k), bank).then_inc(sem["v_q%d0" % k], 1)
        for c in subs:
            for k in (0, 1):
                wait("g", "v_q%d0" % k, 1)
                send(mine[k], sb(T.x2, c), sb(T.p2, c, k * CW), "r_x2%d" % c)
        wait("sc", "sent", sent[0])
        load("sc", T.wdo[:], T.wd[:], "ld_o")
        wait("g", "ld_o", 16)
        for c in (A, B):
            send(c, T.d2[:], T.wdo[:], "r_d2")
        for k, qn in ((0, "sy"), (1, "sc")):
            store(qn, k, hb(T.land, k), [("r_ln%d%d" % (k, c), eng(mine[k], rank)) for c in subs])
        wait("g", "sent", sent[0])
        return

    if role == 3:
        g.vector.memset(T.zeros[:], 0.0).then_inc(sem.z, 1)
        for k, qn in ((0, "sy"), (1, "sc")):
            load(qn, hb(T.xs, k), hb(T.x, k), "ld_x%d" % k)
        for c in subs:
            for k in (0, 1):
                wait("g", "ld_x%d" % k, 16)
                send(mine[k], sb(T.x3, c), sb(T.xs, c, k * CW), "r_x3%d" % c)
        wait("sc", "sent", sent[0])
        load("sc", T.wdo[:], T.wd[:], "ld_o")
        for c in subs:
            for k in (0, 1):
                mm("lf%d" % k, c, T.wdo[:, 0:128], T.xs, k * CW, True, False, [("ld_o", 16), ("ld_x%d" % k, 16)])
        for c in subs:
            for k in (0, 1):
                mm("lf%d" % k, c, T.wdo[:, 128:256], T.land, k * CW, False, True,
                   [("r_ln%d%d" % (k, c), eng(mine[k], rank))])
                relu("lf%d" % k, c, T.yo, k * CW)
        for k, qn in ((0, "sy"), (1, "sc")):
            store(qn, k, hb(T.yo, k), done("lf%d" % k))
        wait("g", "sent", sent[0])
        return

    k = role
    other = mine[1 - k]
    partner, cable = rackmate(q) + k, cabled(q) + k
    pair_root = q - q % half
    in_low = pair_root == low
    own_node = q != pair_root
    sqn = "sq" if own_node else ("s8" if in_low else "rt")
    D8, E8 = T.wt[:, 0:128], T.wt[:, 128:256]
    U2, V2 = T.wt[:, 256:384], T.wt[:, 384:512]
    U3, V3 = T.wt[:, 512:640], T.wt[:, 640:768]
    w3 = T.wt[:, W3[0]:W3[1]]

    g.vector.memset(T.zeros[:], 0.0).then_inc(sem.z, 1)
    if k == 0:
        load("sc", T.wus[:, 0:256], T.wu[:, 0:256], "ld_w0")
        load("sc", T.xs[:], T.x[:], "ld_x")
        if rank == top:
            load("sy", T.wt[:, 256:768], T.wu[:, 512:1024], "ld_wt")
        elif rank == low:
            load("sy", T.wt[:, 256:512], T.wu[:, 512:768], "ld_wt")
            load("sy", T.wt[:, 0:256], T.wd[:], "ld_w8")
        load("sy", T.wus[:, 256:512], T.wu[:, 256:512], "ld_w1")
        if own_node:
            load("sy", T.wds[:], T.wd[:], "ld_d")
    else:
        load("sy", T.xs[:], T.x[:], "ld_x")
        load("sc", T.wdo[:], T.wd[:], "ld_o")

    def via(s):
        for R, cc, cols, dests, sm, ld in plan:
            if sm == s and rank in dests:
                return [(s, pop(topo.mask(cc, core)))]
        return None

    have_w0 = [("ld_w0", 16)] if k == 0 else [("r_w0", eng(A, rank))]
    have_w1 = [("ld_w1", 16)] if k == 0 else [("r_w1", eng(A, rank))]
    have2 = [("ld_wt", 16)] if rank == pair_root else via("r_w2t")
    if rank == top:
        have3 = [("ld_wt", 16)]
    elif via("r_w3"):
        have3 = via("r_w3")
    elif q == near:
        have3 = [("r_w3", eng(top, rank))]
    else:
        have3 = [("r_w3", eng(near + k, rank))]
    have8 = ([("ld_w8", 16)] if rank == low else via("r_w8")) if in_low else []
    haved = [("ld_d", 16)] if k == 0 else [("r_wds", eng(A, rank))]

    def v(node, c):
        return ("v_%s%d" % (node, c), 1)

    U0, V0, U1, V1 = (T.wus[:, 128 * i:128 * (i + 1)] for i in range(4))
    if k == 0:
        wait("g", "ld_w0", 16)
        send(B, V0, V0, "r_w0")
        for R, cc, cols, dests, s, ld in plan:
            if R == rank:
                wait("g", ld, 16)
                put(cc, T.wt[:, cols[0]:cols[1]], T.wt[:, cols[0]:cols[1]], "r_c", side(R, cc))
        wait("g", *v("p0", 0))
        send(B, sb(T.xo, 0), sb(T.p0, 0), "r_xo0")
        wait("g", "ld_w1", 16)
        send(B, T.wus[:, 256:512], T.wus[:, 256:512], "r_w1")
        wait("g", *v("p0", 1))
        send(B, sb(T.xo, 1), sb(T.p0, 1), "r_xo1")
        if rank == top:
            send(near, w3, w3, "r_w3")
    else:
        wait("g", "ld_x", 16)
        send(A, T.xo[:], hb(T.xs, 0), "r_xo0")
    for c in subs:
        wait("g", *v("h", c))
        send(partner, sb(T.hp, c), sb(T.h, c), "r_hp%d" % c)
    if q == near:
        for s, n_ in have3:
            wait("g", s, n_)
        send(far + k, w3, w3, "r_w3")
    if k == 0 and own_node:
        wait("g", "ld_d", 16)
        send(B, T.wds[:], T.wds[:], "r_wds")
    for c in subs:
        wait("g", *v("ar", c))
        send(cable, sb(T.ao, c), sb(T.ar, c), "r_ao%d" % c)
    for c in subs:
        wait("g", *v(sqn, c))
        send(other, sb(T.land, c, k * CW), sb(T[sqn], c), "r_land%d" % c)
        wait("g", *v("sp", c))
        send(L3, sb(T.land, c, k * CW), sb(T.sp, c), "r_ln%d%d" % (k, c))
        send(L2, sb(T.land, c, k * CW), sb(T.sp, c), "r_ln%d%d" % (k, c))
    wait("g", "sent", sent[0])

    if k == 0:
        for c in subs:
            mm("p0", c, U0, T.xs, CW, True, True, have_w0 + [("ld_x", 16)])
            wait("dve", "p_p0%d" % c, 1)
            g.vector.tensor_copy(sb(T.p0, c), ps("p0", c)).then_inc(sem["v_p0%d" % c], 1)
        for c in subs:
            mm("a", c, U0, T.xs, 0, True, False, [])
    for c in subs:
        if k == 0:
            mm("a", c, V0, T.xo, 0, False, True, [("r_xo0", eng(B, rank))])
            relu("a", c, T.a)
        else:
            mm("a", c, V0, T.xs, CW, True, True, have_w0 + [("ld_x", 16)])
            addrelu("a", c, T.xo, [("r_xo%d" % c, eng(A, rank))], T.a)
        mm("s2", c, T.v2[:], T.x3, 0, True, True, [("r_v2", eng(L2, rank)), ("r_x3%d" % c, eng(L3, rank))])
        addrelu("s2", c, T.x2, [("r_x2%d" % c, eng(L2, rank))], T.s2)
        mm("h", c, U1, T.a, 0, True, False, have_w1 + [v("a", c)])
        mm("h", c, V1, T.s2, 0, False, True, [v("s2", c)])
        relu("h", c, T.h)
    for c in subs:
        mm("ar", c, V2 if own_node else U2, T.h, 0, True, False,
           have2 + [v("h", c)] + ([v("p0", c)] if k == 0 else []))
    for c in subs:
        mm("ar", c, U2 if own_node else V2, T.hp, 0, False, True, [("r_hp%d" % c, eng(partner, rank))])
        relu("ar", c, T.ar)
    for c in subs:
        mm("rt", c, V3 if in_low else U3, T.ar, 0, True, False, have3 + [v("ar", c)])
        if in_low:
            mm("s8", c, D8, T.ar, 0, True, False, have8)
        if own_node:
            mm("sq", c, T.wds[:, 0:128], T.h, 0, True, False, haved)
        mm("sp", c, T.d2[:, 0:128], T.s2, 0, True, False, [("r_d2", eng(L2, rank))])

    chain = [("rt", U3 if in_low else V3, T.ao, None)]
    if in_low:
        chain.append(("s8", E8, T.rt, "rt"))
    if own_node:
        chain.append(("sq", T.wds[:, 128:256], T[chain[-1][0]], chain[-1][0]))
    chain.append(("sp", T.d2[:, 128:256], T[sqn], sqn))
    order, nxt = [(0, 0), (1, 0)], [2, 0]
    while nxt[0] < len(chain) or nxt[1] < len(chain):
        for c in (1, 0):
            if nxt[c] < len(chain):
                order.append((nxt[c], c))
                nxt[c] += 1
    for i, c in order:
        node, tile, operand, src = chain[i]
        mm(node, c, tile, operand, 0, False, True, [v(src, c)] if src else [("r_ao%d" % c, eng(cable, rank))])
        relu(node, c, T[node])

    if k == 0:
        store("sc", 1, hb(T.land, 1), [("r_land%d" % c, eng(B, rank)) for c in subs])
        store("sy", 0, T[sqn][:], done(sqn) + [("sent", sent[0])])
    else:
        for c in subs:
            mm("lf1", c, T.wdo[:, 0:128], T.xs, CW, True, False, [("ld_o", 16)])
            mm("lf0", c, T.wdo[:, 0:128], T.xs, 0, True, False, [])
        for c in subs:
            mm("lf1", c, T.wdo[:, 128:256], T[sqn], 0, False, True, [])
            relu("lf1", c, T.yo, CW)
        for c in subs:
            mm("lf0", c, T.wdo[:, 128:256], T.land, 0, False, True, [("r_land%d" % c, eng(A, rank))])
            relu("lf0", c, T.yo, 0)
        store("sc", 0, hb(T.yo, 0), done("lf0"))
        store("sy", 1, hb(T.yo, 1), done("lf1") + [("sent", sent[0])])
